import numpy as np
import ml_dtypes


def mxq(x, axis, fmt="e4m3"):
    dtype, down = {"e4m3": (ml_dtypes.float8_e4m3fn, 7), "e5m2": (ml_dtypes.float8_e5m2, 14)}[fmt]
    v = np.moveaxis(np.asarray(x, np.float32).astype(ml_dtypes.bfloat16).astype(np.float64), axis, -1)
    blocks = v.reshape(v.shape[:-1] + (-1, 32))
    amax = np.abs(blocks).max(-1, keepdims=True)
    byte = np.maximum(np.where(amax > 0, np.frexp(amax)[1] - 1 + 127, 0) - down, 1)
    scale = np.exp2(byte - 127.0)
    codes = (blocks / scale).astype(np.float32).astype(dtype).astype(np.float64)
    return np.moveaxis((codes * scale).reshape(v.shape), -1, axis)


WIDE = False


def mx_kscale(k):
    if not WIDE:
        return np.ones(k)
    levels = np.array([10, -10, 5, -5, 0])
    if k % 512:
        return np.exp2(np.random.permutation(np.resize(levels, k // 32))).repeat(32)
    a = np.empty((k // 512, 16))
    for p in range(k // 512):
        a[p, :8] = np.random.permutation(np.resize(levels, 8))
        for g in range(8):
            far = levels[np.abs(levels - a[p, g]) >= 10]
            a[p, g + 8] = far[np.random.randint(len(far))]
    return np.exp2(a.ravel()).repeat(32)


def f64(x):
    return np.asarray(x).astype(np.float64)


def striped(idx):
    return np.tile(idx.reshape(-1, 16).T, (8, 1)).astype(np.uint16)


def unstriped(offs):
    return offs[:16].T.reshape(-1).astype(np.int64)


E2M1 = np.array([0.0, 0.5, 1.0, 1.5, 2.0, 3.0, 4.0, 6.0, -0.0, -0.5, -1.0, -1.5, -2.0, -3.0, -4.0, -6.0])


def pack_weight(w, fmt):
    k, n = w.shape
    w = f64(np.asarray(w, np.float32).astype(ml_dtypes.bfloat16)).reshape(k // 32, 32, n)
    amax = np.abs(w).max(1)
    if fmt == "e4m3":
        byte = np.frexp(amax)[1] - 1 + 127 - 7
    else:
        mant, ex = np.frexp(amax / 6.0)
        byte = np.where(mant > 0.5, ex, ex - 1) + 127
    byte = np.clip(np.where(amax > 0, byte, 1), 1, 254)
    scaled = (w * np.exp2(127.0 - byte)[:, None, :]).reshape(k, n).astype(np.float32)
    by_word = np.ascontiguousarray(scaled.reshape(k // 512, 128, 4, n).transpose(0, 1, 3, 2))
    if fmt == "e4m3":
        words = by_word.astype(ml_dtypes.float8_e4m3fn).view(np.uint8)
    else:
        c = by_word.astype(ml_dtypes.float4_e2m1fn).view(np.uint8) & 0xF
        words = (c[..., 0::2] | (c[..., 1::2] << 4)).reshape(k // 512, 128, 2 * n)
    return np.ascontiguousarray(words), np.ascontiguousarray(byte.astype(np.uint8).reshape(k // 512, 16, n))


def unpack_weight(words, scales, fmt):
    g, _, n = scales.shape
    words = np.ascontiguousarray(words).reshape(g, 128, n, -1)
    if fmt == "e4m3":
        vals = words.view(ml_dtypes.float8_e4m3fn).astype(np.float64)
    else:
        nib = np.empty((g, 128, n, 4), np.uint8)
        nib[..., 0::2] = words & 0xF
        nib[..., 1::2] = words >> 4
        vals = E2M1[nib]
    vals = vals * np.repeat(np.exp2(scales.astype(np.float64) - 127.0), 8, axis=1)[..., None]
    return vals.transpose(0, 1, 3, 2).reshape(g * 512, n)


def relu(v):
    return np.maximum(v, 0.0)


K, T, E, C, N = 1024, 2048, 6, 256, 128
K8 = 512


def by_expert(wq, xq):
    return np.concatenate([wq[e].T @ xq[:, e * C:(e + 1) * C] for e in range(E)], axis=1)


def setup_inputs():
    n = np.random.standard_normal
    s = mx_kscale(K)[:, None]
    w = n((E, K, N)) / np.sqrt(K) / s[None]
    w8 = [pack_weight(m[:K8], "e4m3") for m in w]
    w4 = [pack_weight(m[K8:], "e2m1") for m in w]
    return {
        "xT": (n((K, T)) * s).astype(np.float32),
        "w8_words": np.stack([m[0] for m in w8]),
        "w8_scales": np.stack([m[1] for m in w8]),
        "w4_words": np.stack([m[0] for m in w4]),
        "w4_scales": np.stack([m[1] for m in w4]),
        "b": (0.3 * n((N, E))).astype(np.float32),
        "gate": np.tile(np.random.uniform(0.2, 1.0, E * C), (N, 1)).astype(np.float32),
        "offs": striped(np.random.permutation(T)[:E * C]),
        "dst": striped(np.random.permutation(T)[:E * C]),
    }


def reference(xT, w8_words, w8_scales, w4_words, w4_scales, b, gate, offs, dst):
    idx = unstriped(offs)
    w = np.stack([np.concatenate([unpack_weight(w8_words[e], w8_scales[e], "e4m3"), unpack_weight(w4_words[e], w4_scales[e], "e2m1")]) for e in range(E)])
    xq = mxq(f64(xT)[:, idx], 0, "e4m3")
    y = by_expert(w, xq)
    y = relu(y + np.repeat(f64(b), C, axis=1))
    out = np.zeros((N, T))
    out[:, unstriped(dst)] = f64(gate) * y
    return out

@@ -1,0 +1,156 @@
+from contextlib import ExitStack
+
+import concourse.mybir as mybir
+
+K, T, E, C, N = 1024, 2048, 6, 256, 128
+S = E * C
+
+F32 = mybir.dt.float32
+BF16 = mybir.dt.bfloat16
+I32 = mybir.dt.int32
+U32 = mybir.dt.uint32
+U16 = mybir.dt.uint16
+U8 = mybir.dt.uint8
+E4M3X4 = mybir.dt.float8_e4m3fn_x4
+E2M1X4 = mybir.dt.float4_e2m1fn_x4
+COPY = mybir.ActivationFunctionType.Copy
+RELU = mybir.ActivationFunctionType.Relu
+MULT = mybir.AluOpType.mult
+
+FLOPS = 2 * K * N * S
+
+P = 128
+PACK = 4
+K_PASS = P * PACK
+PIECE = 512
+CHUNKS = (
+    (0, 0, 512), (0, 512, 512), (0, 1024, 512), (0, 1536, 512),
+    (1, 0, 512), (1, 512, 512), (1, 1024, 512), (1, 1536, 256), (1, 1792, 256),
+)
+PLANE_ROW = (4, 0)
+
+
+def tile_moe_two_lin_relu_kernel(
+    tc, xT, w8_words, w8_scales, w4_words, w4_scales, b, gate, offs, dst, out
+):
+    nc = tc.nc
+    with ExitStack() as ctx:
+        keep = ctx.enter_context(tc.tile_pool(name="keep", bufs=1))
+        stage = ctx.enter_context(tc.tile_pool(name="stage", bufs=len(CHUNKS)))
+        work = ctx.enter_context(tc.tile_pool(name="work", bufs=E))
+        psum = ctx.enter_context(tc.psum_pool(name="psum", bufs=E))
+
+        offs_sb = keep.tile([P, S // 16], U16, name="offs_sb")
+        dst_sb = keep.tile([P, S // 16], U16, name="dst_sb")
+        words = [keep.tile([P, T], U32, name=f"words{a}", align_bytes=64) for a in range(2)]
+        planes = keep.tile([P, T], U8, name="planes", align_bytes=64)
+        words_g = [keep.tile([P, S], U32, name=f"words_g{a}", align_bytes=64) for a in range(2)]
+        planes_g = keep.tile([P, S], U8, name="planes_g", align_bytes=64)
+        w8_sb = keep.tile([P, E, 4 * N], U8, name="w8_sb", align_bytes=64)
+        w4_sb = keep.tile([P, E, 2 * N], U8, name="w4_sb", align_bytes=64)
+        w_planes = keep.tile([P, E, N], U8, name="w_planes", align_bytes=64)
+        bias = keep.tile([P, E], F32, name="bias")
+        gate_sb = keep.tile([P, S], F32, name="gate_sb")
+        out_sb = keep.tile([P, T], F32, name="out_sb")
+
+        nc.gpsimd.memset(w_planes[:].bitcast(I32), 0)
+        nc.gpsimd.memset(planes[:], 0)
+        nc.vector.memset(out_sb[:], 0.0)
+        for q in range(4):
+            nc.scalar.dma_start(
+                out=w_planes[32 * q + 4 : 32 * q + 8].bitcast(I32),
+                in_=w8_scales[:, :, 4 * q : 4 * q + 4, :].rearrange("e a q n -> q (e a) n").bitcast(I32),
+            )
+            nc.scalar.dma_start(
+                out=w_planes[32 * q : 32 * q + 4].bitcast(I32),
+                in_=w4_scales[:, :, 4 * q : 4 * q + 4, :].rearrange("e a q n -> q (e a) n").bitcast(I32),
+            )
+
+        raws = []
+        for i, (a, c0, width) in enumerate(CHUNKS):
+            raw = stage.tile([P, PACK, width], F32, name="raw")
+            rows = xT[a * K_PASS : (a + 1) * K_PASS, c0 : c0 + width]
+            nc.sync.dma_start(out=raw[:], in_=rows.rearrange("(p j) w -> p j w", j=PACK))
+            raws.append(raw)
+            if i == 0:
+                nc.sync.dma_start(offs_sb[:], offs)
+        nc.sync.dma_start(out=w8_sb[:].bitcast(I32), in_=w8_words.rearrange("e a p n r -> p (e a) (n r)").bitcast(I32))
+        nc.sync.dma_start(out=w4_sb[:].bitcast(I32), in_=w4_words.rearrange("e a p n -> p (e a) n").bitcast(I32))
+        nc.sync.dma_start(out=bias[:], in_=b)
+        nc.sync.dma_start(out=gate_sb[:], in_=gate)
+        nc.sync.dma_start(dst_sb[:], dst)
+
+        grouped = []
+
+        def interleave(i):
+            width = CHUNKS[i][2]
+            cut = 352 if width == 512 else 96
+            g = stage.tile([P, width, PACK], BF16, name="g", align_bytes=64)
+            for lo, hi, on_scalar in ((0, cut, True), (cut, width, False)):
+                dst_view = g[:, lo:hi, :].rearrange("p (c i) j -> p c j i", i=4)
+                src_view = raws[i][:, :, lo:hi].rearrange("p j (c i) -> p c j i", i=4)
+                if on_scalar:
+                    nc.scalar.activation(dst_view, src_view, COPY)
+                else:
+                    nc.vector.tensor_copy(out=dst_view, in_=src_view)
+            grouped.append(g)
+
+        def quantize(i):
+            a, c0, width = CHUNKS[i]
+            nc.vector.quantize_mx(
+                out=words[a][:, c0 : c0 + width].bitcast(E4M3X4),
+                scales=planes[PLANE_ROW[a] : P, c0 : c0 + width],
+                in_=grouped[i][:].rearrange("p c j -> p (c j)"),
+            )
+
+        def gather(target, source, lo, hi):
+            nc.vector.tensor_copy(target[:, lo:hi], source[:].indirect(offs_sb[:, lo // 16 : hi // 16]))
+
+        interleave(0)
+        for i in range(1, 4):
+            interleave(i)
+            quantize(i - 1)
+        quantize(3)
+        for i in range(4, 7):
+            interleave(i)
+            gather(words_g[0], words[0], (i - 4) * PIECE, (i - 3) * PIECE)
+            quantize(i)
+        interleave(7)
+        interleave(8)
+        quantize(7)
+        quantize(8)
+
+        for lo, hi in ((0, 1536),):
+            gather(words_g[1], words[1], lo, hi)
+        acts = keep.tile([P, S], F32, name="acts")
+        for lo, hi in ((0, 512), (512, 1536)):
+            gather(planes_g, planes, lo, hi)
+            for e in range(lo // C, hi // C):
+                acc = psum.tile([P, C], F32, name="acc")
+                for h in range(0, C, 128):
+                    cols = slice(e * C + h, e * C + h + 128)
+                    nc.tensor.matmul_mx(
+                        out=acc[:, h : h + 128],
+                        lhsT=w8_sb[:, e, :].bitcast(E4M3X4),
+                        lhsT_scale=w_planes[PLANE_ROW[0] : P, e, :],
+                        rhs=words_g[0][:, cols].bitcast(E4M3X4),
+                        rhs_scale=planes_g[PLANE_ROW[0] : P, cols],
+                        start=True,
+                        stop=False,
+                    )
+                    nc.tensor.matmul_mx(
+                        out=acc[:, h : h + 128],
+                        lhsT=w4_sb[:, e, :].bitcast(E2M1X4),
+                        lhsT_scale=w_planes[PLANE_ROW[1] : P, e, :],
+                        rhs=words_g[1][:, cols].bitcast(E4M3X4),
+                        rhs_scale=planes_g[PLANE_ROW[1] : P, cols],
+                        start=False,
+                        stop=True,
+                    )
+                nc.scalar.activation(acts[:, e * C : (e + 1) * C], acc[:], RELU, bias=bias[:, e : e + 1])
+
+        for lo, hi in ((0, 512), (512, 1024), (1024, 1536)):
+            nc.vector.tensor_tensor(
+                out_sb[:].indirect(dst_sb[:, lo // 16 : hi // 16]), acts[:, lo:hi], gate_sb[:, lo:hi], MULT
+            )
+        nc.sync.dma_start(out=out, in_=out_sb[:])

@@ -54,14 +54,14 @@ def tile_moe_two_lin_relu_kernel(
         out_sb = keep.tile([P, T], F32, name="out_sb")
 
         nc.gpsimd.memset(w_planes[:].bitcast(I32), 0)
-        nc.gpsimd.memset(planes[:], 0)
+        nc.gpsimd.memset(planes[:].bitcast(I32), 0)
         nc.vector.memset(out_sb[:], 0.0)
         for q in range(4):
-            nc.scalar.dma_start(
+            nc.gpsimd.dma_start(
                 out=w_planes[32 * q + 4 : 32 * q + 8].bitcast(I32),
                 in_=w8_scales[:, :, 4 * q : 4 * q + 4, :].rearrange("e a q n -> q (e a) n").bitcast(I32),
             )
-            nc.scalar.dma_start(
+            nc.gpsimd.dma_start(
                 out=w_planes[32 * q : 32 * q + 4].bitcast(I32),
                 in_=w4_scales[:, :, 4 * q : 4 * q + 4, :].rearrange("e a q n -> q (e a) n").bitcast(I32),
             )
@@ -77,8 +77,8 @@ def tile_moe_two_lin_relu_kernel(
         nc.sync.dma_start(out=w8_sb[:].bitcast(I32), in_=w8_words.rearrange("e a p n r -> p (e a) (n r)").bitcast(I32))
         nc.sync.dma_start(out=w4_sb[:].bitcast(I32), in_=w4_words.rearrange("e a p n -> p (e a) n").bitcast(I32))
         nc.sync.dma_start(out=bias[:], in_=b)
-        nc.sync.dma_start(out=gate_sb[:], in_=gate)
         nc.sync.dma_start(dst_sb[:], dst)
+        nc.sync.dma_start(out=gate_sb[:], in_=gate)
 
         grouped = []
 
@@ -149,8 +149,8 @@ def tile_moe_two_lin_relu_kernel(
                     )
                 nc.scalar.activation(acts[:, e * C : (e + 1) * C], acc[:], RELU, bias=bias[:, e : e + 1])
 
-        for lo, hi in ((0, 512), (512, 1024), (1024, 1536)):
-            nc.vector.tensor_tensor(
-                out_sb[:].indirect(dst_sb[:, lo // 16 : hi // 16]), acts[:, lo:hi], gate_sb[:, lo:hi], MULT
-            )
+        gated = keep.tile([P, S], F32, name="gated")
+        for lo, hi in ((0, 512), (512, 1536)):
+            nc.vector.tensor_tensor(gated[:, lo:hi], acts[:, lo:hi], gate_sb[:, lo:hi], MULT)
+            nc.vector.tensor_copy(out_sb[:].indirect(dst_sb[:, lo // 16 : hi // 16]), gated[:, lo:hi])
         nc.sync.dma_start(out=out, in_=out_sb[:])

@@ -23,9 +23,14 @@ P = 128
 PACK = 4
 K_PASS = P * PACK
 PIECE = 512
-CHUNKS = (
-    (0, 0, 512), (0, 512, 512), (0, 1024, 512), (0, 1536, 512),
-    (1, 0, 512), (1, 512, 512), (1, 1024, 512), (1, 1536, 256), (1, 1792, 256),
+LOADS = (
+    (0, 0, 1024),
+    (0, 1024, 512),
+    (0, 1536, 512),
+    (1, 0, 1024),
+    (1, 1024, 512),
+    (1, 1536, 256),
+    (1, 1792, 256),
 )
 PLANE_ROW = (4, 0)
 
@@ -36,7 +41,7 @@ def tile_moe_two_lin_relu_kernel(
     nc = tc.nc
     with ExitStack() as ctx:
         keep = ctx.enter_context(tc.tile_pool(name="keep", bufs=1))
-        stage = ctx.enter_context(tc.tile_pool(name="stage", bufs=len(CHUNKS)))
+        stage = ctx.enter_context(tc.tile_pool(name="stage", bufs=len(LOADS)))
         work = ctx.enter_context(tc.tile_pool(name="work", bufs=E))
         psum = ctx.enter_context(tc.psum_pool(name="psum", bufs=E))
 
@@ -46,6 +51,7 @@ def tile_moe_two_lin_relu_kernel(
         planes = keep.tile([P, T], U8, name="planes", align_bytes=64)
         words_g = [keep.tile([P, S], U32, name=f"words_g{a}", align_bytes=64) for a in range(2)]
         planes_g = keep.tile([P, S], U8, name="planes_g", align_bytes=64)
+        grouped = [keep.tile([P, T, PACK], BF16, name=f"grouped{a}", align_bytes=64) for a in range(2)]
         w8_sb = keep.tile([P, E, 4 * N], U8, name="w8_sb", align_bytes=64)
         w4_sb = keep.tile([P, E, 2 * N], U8, name="w4_sb", align_bytes=64)
         w_planes = keep.tile([P, E, N], U8, name="w_planes", align_bytes=64)
@@ -67,8 +73,8 @@ def tile_moe_two_lin_relu_kernel(
             )
 
         raws = []
-        for i, (a, c0, width) in enumerate(CHUNKS):
-            raw = stage.tile([P, PACK, width], F32, name="raw")
+        for i, (a, c0, width) in enumerate(LOADS):
+            raw = keep.tile([P, PACK, width], F32, name=f"raw{i}")
             rows = xT[a * K_PASS : (a + 1) * K_PASS, c0 : c0 + width]
             nc.sync.dma_start(out=raw[:], in_=rows.rearrange("(p j) w -> p j w", j=PACK))
             raws.append(raw)
@@ -79,78 +85,86 @@ def tile_moe_two_lin_relu_kernel(
         nc.sync.dma_start(out=bias[:], in_=b)
         nc.sync.dma_start(dst_sb[:], dst)
         nc.sync.dma_start(out=gate_sb[:], in_=gate)
+        acts = keep.tile([P, S], F32, name="acts")
 
-        grouped = []
-
-        def interleave(i):
-            width = CHUNKS[i][2]
-            cut = 352 if width == 512 else 96
-            g = stage.tile([P, width, PACK], BF16, name="g", align_bytes=64)
-            for lo, hi, on_scalar in ((0, cut, True), (cut, width, False)):
-                dst_view = g[:, lo:hi, :].rearrange("p (c i) j -> p c j i", i=4)
-                src_view = raws[i][:, :, lo:hi].rearrange("p j (c i) -> p c j i", i=4)
+        def interleave(i, lo, hi, cut):
+            a, c0, width = LOADS[i]
+            for first, last, on_scalar in ((lo, cut, True), (cut, hi, False)):
+                if first == last:
+                    continue
+                to = grouped[a][:, c0 + first : c0 + last, :].rearrange("p (c i) j -> p c j i", i=4)
+                source = raws[i][:, :, first:last].rearrange("p j (c i) -> p c j i", i=4)
                 if on_scalar:
-                    nc.scalar.activation(dst_view, src_view, COPY)
+                    nc.scalar.activation(to, source, COPY)
                 else:
-                    nc.vector.tensor_copy(out=dst_view, in_=src_view)
-            grouped.append(g)
+                    nc.vector.tensor_copy(out=to, in_=source)
 
-        def quantize(i):
-            a, c0, width = CHUNKS[i]
+        def quantize(a, lo, hi):
             nc.vector.quantize_mx(
-                out=words[a][:, c0 : c0 + width].bitcast(E4M3X4),
-                scales=planes[PLANE_ROW[a] : P, c0 : c0 + width],
-                in_=grouped[i][:].rearrange("p c j -> p (c j)"),
+                out=words[a][:, lo:hi].bitcast(E4M3X4),
+                scales=planes[PLANE_ROW[a] : P, lo:hi],
+                in_=grouped[a][:, lo:hi, :].rearrange("p c j -> p (c j)"),
             )
 
         def gather(target, source, lo, hi):
             nc.vector.tensor_copy(target[:, lo:hi], source[:].indirect(offs_sb[:, lo // 16 : hi // 16]))
 
-        interleave(0)
-        for i in range(1, 4):
-            interleave(i)
-            quantize(i - 1)
-        quantize(3)
-        for i in range(4, 7):
-            interleave(i)
-            gather(words_g[0], words[0], (i - 4) * PIECE, (i - 3) * PIECE)
-            quantize(i)
-        interleave(7)
-        interleave(8)
-        quantize(7)
-        quantize(8)
+        def expert(e):
+            acc = psum.tile([P, C], F32, name="acc")
+            for h in range(0, C, 128):
+                cols = slice(e * C + h, e * C + h + 128)
+                nc.tensor.matmul_mx(
+                    out=acc[:, h : h + 128],
+                    lhsT=w8_sb[:, e, :].bitcast(E4M3X4),
+                    lhsT_scale=w_planes[PLANE_ROW[0] : P, e, :],
+                    rhs=words_g[0][:, cols].bitcast(E4M3X4),
+                    rhs_scale=planes_g[PLANE_ROW[0] : P, cols],
+                    start=True,
+                    stop=False,
+                )
+                nc.tensor.matmul_mx(
+                    out=acc[:, h : h + 128],
+                    lhsT=w4_sb[:, e, :].bitcast(E2M1X4),
+                    lhsT_scale=w_planes[PLANE_ROW[1] : P, e, :],
+                    rhs=words_g[1][:, cols].bitcast(E4M3X4),
+                    rhs_scale=planes_g[PLANE_ROW[1] : P, cols],
+                    start=False,
+                    stop=True,
+                )
+            nc.scalar.activation(acts[:, e * C : (e + 1) * C], acc[:], RELU, bias=bias[:, e : e + 1])
 
-        for lo, hi in ((0, 1536),):
-            gather(words_g[1], words[1], lo, hi)
-        acts = keep.tile([P, S], F32, name="acts")
-        for lo, hi in ((0, 512), (512, 1536)):
-            gather(planes_g, planes, lo, hi)
-            for e in range(lo // C, hi // C):
-                acc = psum.tile([P, C], F32, name="acc")
-                for h in range(0, C, 128):
-                    cols = slice(e * C + h, e * C + h + 128)
-                    nc.tensor.matmul_mx(
-                        out=acc[:, h : h + 128],
-                        lhsT=w8_sb[:, e, :].bitcast(E4M3X4),
-                        lhsT_scale=w_planes[PLANE_ROW[0] : P, e, :],
-                        rhs=words_g[0][:, cols].bitcast(E4M3X4),
-                        rhs_scale=planes_g[PLANE_ROW[0] : P, cols],
-                        start=True,
-                        stop=False,
-                    )
-                    nc.tensor.matmul_mx(
-                        out=acc[:, h : h + 128],
-                        lhsT=w4_sb[:, e, :].bitcast(E2M1X4),
-                        lhsT_scale=w_planes[PLANE_ROW[1] : P, e, :],
-                        rhs=words_g[1][:, cols].bitcast(E4M3X4),
-                        rhs_scale=planes_g[PLANE_ROW[1] : P, cols],
-                        start=False,
-                        stop=True,
-                    )
-                nc.scalar.activation(acts[:, e * C : (e + 1) * C], acc[:], RELU, bias=bias[:, e : e + 1])
+        def scatter(lo, hi):
+            nc.vector.tensor_tensor(
+                out_sb[:].indirect(dst_sb[:, lo // 16 : hi // 16]), acts[:, lo:hi], gate_sb[:, lo:hi], MULT
+            )
 
-        gated = keep.tile([P, S], F32, name="gated")
-        for lo, hi in ((0, 512), (512, 1536)):
-            nc.vector.tensor_tensor(gated[:, lo:hi], acts[:, lo:hi], gate_sb[:, lo:hi], MULT)
-            nc.vector.tensor_copy(out_sb[:].indirect(dst_sb[:, lo // 16 : hi // 16]), gated[:, lo:hi])
+        interleave(0, 0, 512, 256)
+        interleave(0, 512, 1024, 768)
+        quantize(0, 0, 512)
+        quantize(0, 512, 1024)
+        interleave(1, 0, 512, 256)
+        quantize(0, 1024, 1536)
+        interleave(2, 0, 256, 96)
+        interleave(2, 256, 512, 352)
+        quantize(0, 1536, 1792)
+        quantize(0, 1792, T)
+        gather(words_g[0], words[0], 0, S)
+        interleave(3, 0, 512, 352)
+        interleave(3, 512, 1024, 832)
+        quantize(1, 0, 512)
+        interleave(4, 0, 512, 256)
+        quantize(1, 512, 1024)
+        interleave(5, 0, 256, 96)
+        quantize(1, 1024, 1536)
+        interleave(6, 0, 256, 96)
+        quantize(1, 1536, 1792)
+        quantize(1, 1792, T)
+        gather(words_g[1], words[1], 0, S)
+        gather(planes_g, planes, 0, 256)
+        expert(0)
+        gather(planes_g, planes, 256, S)
+        for e in range(1, E):
+            expert(e)
+        for lo, hi in ((0, 256), (256, 512), (512, 1024), (1024, 1536)):
+            scatter(lo, hi)
         nc.sync.dma_start(out=out, in_=out_sb[:])

@@ -28,8 +28,7 @@ LOADS = (
     (0, 1024, 512),
     (0, 1536, 512),
     (1, 0, 1024),
-    (1, 1024, 512),
-    (1, 1536, 256),
+    (1, 1024, 768),
     (1, 1792, 256),
 )
 PLANE_ROW = (4, 0)
@@ -146,17 +145,16 @@ def tile_moe_two_lin_relu_kernel(
         quantize(0, 1024, 1536)
         interleave(2, 0, 256, 96)
         interleave(2, 256, 512, 352)
-        quantize(0, 1536, 1792)
-        quantize(0, 1792, T)
+        quantize(0, 1536, T)
         gather(words_g[0], words[0], 0, S)
         interleave(3, 0, 512, 352)
         interleave(3, 512, 1024, 832)
         quantize(1, 0, 512)
-        interleave(4, 0, 512, 256)
         quantize(1, 512, 1024)
-        interleave(5, 0, 256, 96)
+        interleave(4, 0, 512, 272)
+        interleave(4, 512, 768, 640)
         quantize(1, 1024, 1536)
-        interleave(6, 0, 256, 96)
+        interleave(5, 0, 256, 96)
         quantize(1, 1536, 1792)
         quantize(1, 1792, T)
         gather(words_g[1], words[1], 0, S)
@@ -165,6 +163,6 @@ def tile_moe_two_lin_relu_kernel(
         gather(planes_g, planes, 256, S)
         for e in range(1, E):
             expert(e)
-        for lo, hi in ((0, 256), (256, 512), (512, 1024), (1024, 1536)):
+        for lo, hi in ((0, 256), (256, 512), (512, S)):
             scatter(lo, hi)
         nc.sync.dma_start(out=out, in_=out_sb[:])

from contextlib import ExitStack

import concourse.mybir as mybir

K, T, E, C, N = 1024, 2048, 6, 256, 128
S = E * C

F32 = mybir.dt.float32
BF16 = mybir.dt.bfloat16
I32 = mybir.dt.int32
U32 = mybir.dt.uint32
U16 = mybir.dt.uint16
U8 = mybir.dt.uint8
E4M3X4 = mybir.dt.float8_e4m3fn_x4
E2M1X4 = mybir.dt.float4_e2m1fn_x4
COPY = mybir.ActivationFunctionType.Copy
RELU = mybir.ActivationFunctionType.Relu
MULT = mybir.AluOpType.mult

FLOPS = 2 * K * N * S

P = 128
PACK = 4
K_PASS = P * PACK
PIECE = 512
LOADS = (
    (0, 0, 1024),
    (0, 1024, 512),
    (0, 1536, 512),
    (1, 0, 1024),
    (1, 1024, 768),
    (1, 1792, 256),
)
PLANE_ROW = (4, 0)


def tile_moe_two_lin_relu_kernel(
    tc, xT, w8_words, w8_scales, w4_words, w4_scales, b, gate, offs, dst, out
):
    nc = tc.nc
    with ExitStack() as ctx:
        keep = ctx.enter_context(tc.tile_pool(name="keep", bufs=1))
        stage = ctx.enter_context(tc.tile_pool(name="stage", bufs=len(LOADS)))
        work = ctx.enter_context(tc.tile_pool(name="work", bufs=E))
        psum = ctx.enter_context(tc.psum_pool(name="psum", bufs=E))

        offs_sb = keep.tile([P, S // 16], U16, name="offs_sb")
        dst_sb = keep.tile([P, S // 16], U16, name="dst_sb")
        words = [keep.tile([P, T], U32, name=f"words{a}", align_bytes=64) for a in range(2)]
        planes = keep.tile([P, T], U8, name="planes", align_bytes=64)
        words_g = [keep.tile([P, S], U32, name=f"words_g{a}", align_bytes=64) for a in range(2)]
        planes_g = keep.tile([P, S], U8, name="planes_g", align_bytes=64)
        grouped = [keep.tile([P, T, PACK], BF16, name=f"grouped{a}", align_bytes=64) for a in range(2)]
        w8_sb = keep.tile([P, E, 4 * N], U8, name="w8_sb", align_bytes=64)
        w4_sb = keep.tile([P, E, 2 * N], U8, name="w4_sb", align_bytes=64)
        w_planes = keep.tile([P, E, N], U8, name="w_planes", align_bytes=64)
        bias = keep.tile([P, E], F32, name="bias")
        gate_sb = keep.tile([P, S], F32, name="gate_sb")
        out_sb = keep.tile([P, T], F32, name="out_sb")

        nc.gpsimd.memset(w_planes[:].bitcast(I32), 0)
        nc.gpsimd.memset(planes[:].bitcast(I32), 0)
        nc.vector.memset(out_sb[:], 0.0)
        for q in range(4):
            nc.gpsimd.dma_start(
                out=w_planes[32 * q + 4 : 32 * q + 8].bitcast(I32),
                in_=w8_scales[:, :, 4 * q : 4 * q + 4, :].rearrange("e a q n -> q (e a) n").bitcast(I32),
            )
            nc.gpsimd.dma_start(
                out=w_planes[32 * q : 32 * q + 4].bitcast(I32),
                in_=w4_scales[:, :, 4 * q : 4 * q + 4, :].rearrange("e a q n -> q (e a) n").bitcast(I32),
            )

        raws = []
        for i, (a, c0, width) in enumerate(LOADS):
            raw = keep.tile([P, PACK, width], F32, name=f"raw{i}")
            rows = xT[a * K_PASS : (a + 1) * K_PASS, c0 : c0 + width]
            nc.sync.dma_start(out=raw[:], in_=rows.rearrange("(p j) w -> p j w", j=PACK))
            raws.append(raw)
            if i == 0:
                nc.sync.dma_start(offs_sb[:], offs)
        nc.sync.dma_start(out=w8_sb[:].bitcast(I32), in_=w8_words.rearrange("e a p n r -> p (e a) (n r)").bitcast(I32))
        nc.sync.dma_start(out=w4_sb[:].bitcast(I32), in_=w4_words.rearrange("e a p n -> p (e a) n").bitcast(I32))
        nc.sync.dma_start(out=bias[:], in_=b)
        nc.sync.dma_start(dst_sb[:], dst)
        nc.sync.dma_start(out=gate_sb[:], in_=gate)
        acts = keep.tile([P, S], F32, name="acts")

        def interleave(i, lo, hi, cut):
            a, c0, width = LOADS[i]
            for first, last, on_scalar in ((lo, cut, True), (cut, hi, False)):
                if first == last:
                    continue
                to = grouped[a][:, c0 + first : c0 + last, :].rearrange("p (c i) j -> p c j i", i=4)
                source = raws[i][:, :, first:last].rearrange("p j (c i) -> p c j i", i=4)
                if on_scalar:
                    nc.scalar.activation(to, source, COPY)
                else:
                    nc.vector.tensor_copy(out=to, in_=source)

        def quantize(a, lo, hi):
            nc.vector.quantize_mx(
                out=words[a][:, lo:hi].bitcast(E4M3X4),
                scales=planes[PLANE_ROW[a] : P, lo:hi],
                in_=grouped[a][:, lo:hi, :].rearrange("p c j -> p (c j)"),
            )

        def gather(target, source, lo, hi):
            nc.vector.tensor_copy(target[:, lo:hi], source[:].indirect(offs_sb[:, lo // 16 : hi // 16]))

        def expert(e):
            acc = psum.tile([P, C], F32, name="acc")
            for h in range(0, C, 128):
                cols = slice(e * C + h, e * C + h + 128)
                nc.tensor.matmul_mx(
                    out=acc[:, h : h + 128],
                    lhsT=w8_sb[:, e, :].bitcast(E4M3X4),
                    lhsT_scale=w_planes[PLANE_ROW[0] : P, e, :],
                    rhs=words_g[0][:, cols].bitcast(E4M3X4),
                    rhs_scale=planes_g[PLANE_ROW[0] : P, cols],
                    start=True,
                    stop=False,
                )
                nc.tensor.matmul_mx(
                    out=acc[:, h : h + 128],
                    lhsT=w4_sb[:, e, :].bitcast(E2M1X4),
                    lhsT_scale=w_planes[PLANE_ROW[1] : P, e, :],
                    rhs=words_g[1][:, cols].bitcast(E4M3X4),
                    rhs_scale=planes_g[PLANE_ROW[1] : P, cols],
                    start=False,
                    stop=True,
                )
            nc.scalar.activation(acts[:, e * C : (e + 1) * C], acc[:], RELU, bias=bias[:, e : e + 1])

        def scatter(lo, hi):
            nc.vector.tensor_tensor(
                out_sb[:].indirect(dst_sb[:, lo // 16 : hi // 16]), acts[:, lo:hi], gate_sb[:, lo:hi], MULT
            )

        interleave(0, 0, 512, 256)
        interleave(0, 512, 1024, 768)
        quantize(0, 0, 512)
        quantize(0, 512, 1024)
        interleave(1, 0, 512, 256)
        quantize(0, 1024, 1536)
        interleave(2, 0, 256, 96)
        interleave(2, 256, 512, 352)
        quantize(0, 1536, T)
        gather(words_g[0], words[0], 0, S)
        interleave(3, 0, 512, 352)
        interleave(3, 512, 1024, 832)
        quantize(1, 0, 512)
        quantize(1, 512, 1024)
        interleave(4, 0, 512, 272)
        interleave(4, 512, 768, 640)
        quantize(1, 1024, 1536)
        interleave(5, 0, 256, 96)
        quantize(1, 1536, 1792)
        quantize(1, 1792, T)
        gather(words_g[1], words[1], 0, S)
        gather(planes_g, planes, 0, 256)
        expert(0)
        gather(planes_g, planes, 256, S)
        for e in range(1, E):
            expert(e)
        for lo, hi in ((0, 256), (256, 512), (512, S)):
            scatter(lo, hi)
        nc.sync.dma_start(out=out, in_=out_sb[:])
